import numpy as np
CORES = [74,78,202,206,330,334,458,462]
N = 8
GROUPS = [[0,2,4,6],[1,3,5,7]]
def setup_inputs(rng):
    return {"x": rng.standard_normal((N, 128, 1024), dtype=np.float32)}
def reference(x):
    y = np.empty((N, 128, 1024), x.dtype)
    for g in GROUPS:
        s = x[g].sum(axis=0, dtype=np.float64).astype(x[g].dtype)
        for r in g:
            y[r] = s
    return {"y": y}

@@ -1,0 +1,86 @@
+from concourse.bass import DstId, RemoteDMATransfer
+
+CHUNKS = [(-2, "c", 21), (-1, "c", 21), (1, "c", 22)]
+ROWLEN = 1024
+LOW, HIGH = 0x00FF, 0xFF00
+
+SCRATCH = {}
+SEMAPHORES = ["sent", "sta", "stb"]
+for ci, chunk in enumerate(CHUNKS):
+    for nm in "kgpq":
+        SCRATCH["%s%d" % (nm, ci)] = ("dram", [128, chunk[2] * ROWLEN // 128], "float32")
+    for nm in ("ld", "in", "ps", "su", "sv"):
+        SEMAPHORES.append("%s%d" % (nm, ci))
+
+
+def rank_program(g, core, T, topo):
+    near = [r for r in T.cores
+            if topo.host(r) == topo.host(core) and topo.chip(r) == topo.chip(core) and topo.die(r) == topo.die(core)]
+    if not near:
+        return
+    rank_core = near[0]
+    host = topo.host(core)
+    delta = core - rank_core
+
+    def on_host(c, h):
+        return c + (h - host) * 128
+
+    def dst(d):
+        rid, pid = topo.addr(d, core)
+        return DstId(rid=rid, pnc=pid)
+
+    def partners(outer):
+        if outer == "c":
+            return 3 - host, host ^ 1, host in (0, 1)
+        return host ^ 1, 3 - host, host in (0, 3)
+
+    if delta == 0:
+        rows, r0 = [], 0
+        for d, outer, n in CHUNKS:
+            a, b = (r0, r0 + n), (r0 + n, r0 + 2 * n)
+            rows.append((a, b) if partners(outer)[2] else (b, a))
+            r0 += 2 * n
+        for c, (keep, give) in enumerate(rows):
+            g.sync.dma_start(T["g%d" % c][:], T.x[give[0]:give[1], :]).then_inc(T.sem["ld%d" % c], 16)
+            g.scalar.dma_start(T["k%d" % c][:], T.x[keep[0]:keep[1], :]).then_inc(T.sem["ld%d" % c], 16)
+        for c, (d, outer, n) in enumerate(CHUNKS):
+            o_host = partners(outer)[0]
+            g.wait_ge(T.sem["ld%d" % c], 32)
+            g.remote_dma_fused([
+                RemoteDMATransfer(dst_ids=[dst(on_host(core + d, o_host))], dma_engine_mask=LOW,
+                                  remote_sem=T.sem["in%d" % c], src=T["g%d" % c][:], dst=T["g%d" % c][:], alu_op=0),
+                RemoteDMATransfer(dst_ids=[dst(core + d)], dma_engine_mask=HIGH,
+                                  remote_sem=T.sem["in%d" % c], src=T["k%d" % c][:], dst=T["k%d" % c][:], alu_op=0),
+            ], local_sem=T.sem.sent)
+        for c, (keep, give) in enumerate(rows):
+            g.sync.wait_ge(T.sem["su%d" % c], 8)
+            g.sync.dma_start(T.y[keep[0]:keep[1], :], T["p%d" % c][:]).then_inc(T.sem.sta, 16)
+            g.scalar.wait_ge(T.sem["sv%d" % c], 8)
+            g.scalar.dma_start(T.y[give[0]:give[1], :], T["q%d" % c][:]).then_inc(T.sem.stb, 16)
+        g.wait_ge(T.sem.sent, 16 * len(CHUNKS))
+        g.sync.wait_ge(T.sem.sta, 16 * len(CHUNKS))
+        g.scalar.wait_ge(T.sem.stb, 16 * len(CHUNKS))
+        return
+
+    mine = [c for c, ch in enumerate(CHUNKS) if ch[0] == delta]
+    if not mine:
+        return
+    for c in mine:
+        i_host = partners(CHUNKS[c][1])[1]
+        g.wait_ge(T.sem["in%d" % c], 16)
+        g.remote_dma_fused([
+            RemoteDMATransfer(dst_ids=[dst(on_host(core, i_host))], dma_engine_mask=LOW,
+                              remote_sem=T.sem["ps%d" % c], srcs=[T["k%d" % c][:], T["g%d" % c][:]],
+                              dsts=[T["p%d" % c][:]], alu_op=1),
+        ], local_sem=T.sem.sent)
+    for c in mine:
+        o_host = partners(CHUNKS[c][1])[0]
+        srcs = [T["k%d" % c][:], T["g%d" % c][:], T["p%d" % c][:]]
+        g.wait_ge(T.sem["ps%d" % c], 8)
+        g.remote_dma_fused([
+            RemoteDMATransfer(dst_ids=[dst(on_host(rank_core, o_host))], dma_engine_mask=LOW,
+                              remote_sem=T.sem["sv%d" % c], srcs=srcs, dsts=[T["q%d" % c][:]], alu_op=1),
+            RemoteDMATransfer(dst_ids=[dst(rank_core)], dma_engine_mask=HIGH,
+                              remote_sem=T.sem["su%d" % c], srcs=srcs, dsts=[T["p%d" % c][:]], alu_op=1),
+        ], local_sem=T.sem.sent)
+    g.wait_ge(T.sem.sent, 24 * len(mine))

@@ -1,6 +1,6 @@
 from concourse.bass import DstId, RemoteDMATransfer
 
-CHUNKS = [(-2, "c", 21), (-1, "c", 21), (1, "c", 22)]
+CHUNKS = [(-2, "c", 10), (-1, "c", 10), (1, "c", 11), (-2, "c", 11), (-1, "c", 11), (1, "c", 11)]
 ROWLEN = 1024
 LOW, HIGH = 0x00FF, 0xFF00
 

@@ -1,6 +1,6 @@
 from concourse.bass import DstId, RemoteDMATransfer
 
-CHUNKS = [(-2, "c", 10), (-1, "c", 10), (1, "c", 11), (-2, "c", 11), (-1, "c", 11), (1, "c", 11)]
+CHUNKS = [(-2, "s", 10), (-1, "s", 10), (1, "s", 11), (-2, "s", 11), (-1, "s", 11), (1, "s", 11)]
 ROWLEN = 1024
 LOW, HIGH = 0x00FF, 0xFF00
 

@@ -1,26 +1,23 @@
 from concourse.bass import DstId, RemoteDMATransfer
 
-CHUNKS = [(-2, "s", 10), (-1, "s", 10), (1, "s", 11), (-2, "s", 11), (-1, "s", 11), (1, "s", 11)]
+CHUNKS = [(2, -2, "s", 10), (2, 1, "s", 10), (4, -2, "s", 11), (4, 1, "s", 11), (0, -2, "s", 11), (0, 1, "s", 11)]
 ROWLEN = 1024
-LOW, HIGH = 0x00FF, 0xFF00
 
 SCRATCH = {}
 SEMAPHORES = ["sent", "sta", "stb"]
 for ci, chunk in enumerate(CHUNKS):
     for nm in "kgpq":
-        SCRATCH["%s%d" % (nm, ci)] = ("dram", [128, chunk[2] * ROWLEN // 128], "float32")
+        SCRATCH["%s%d" % (nm, ci)] = ("dram", [128, chunk[3] * ROWLEN // 128], "float32")
     for nm in ("ld", "in", "ps", "su", "sv"):
         SEMAPHORES.append("%s%d" % (nm, ci))
 
 
+def masks(dchip):
+    return (0x00FF, 0xFF00, 8) if dchip == 0 else (0x000F, 0x00F0, 4)
+
+
 def rank_program(g, core, T, topo):
-    near = [r for r in T.cores
-            if topo.host(r) == topo.host(core) and topo.chip(r) == topo.chip(core) and topo.die(r) == topo.die(core)]
-    if not near:
-        return
-    rank_core = near[0]
     host = topo.host(core)
-    delta = core - rank_core
 
     def on_host(c, h):
         return c + (h - host) * 128
@@ -34,53 +31,62 @@ def rank_program(g, core, T, topo):
             return 3 - host, host ^ 1, host in (0, 1)
         return host ^ 1, 3 - host, host in (0, 3)
 
-    if delta == 0:
-        rows, r0 = [], 0
-        for d, outer, n in CHUNKS:
+    if T.rank_of(core) is not None:
+        rows, r0, sent = [], 0, 0
+        for dc, d, outer, n in CHUNKS:
             a, b = (r0, r0 + n), (r0 + n, r0 + 2 * n)
             rows.append((a, b) if partners(outer)[2] else (b, a))
             r0 += 2 * n
         for c, (keep, give) in enumerate(rows):
             g.sync.dma_start(T["g%d" % c][:], T.x[give[0]:give[1], :]).then_inc(T.sem["ld%d" % c], 16)
             g.scalar.dma_start(T["k%d" % c][:], T.x[keep[0]:keep[1], :]).then_inc(T.sem["ld%d" % c], 16)
-        for c, (d, outer, n) in enumerate(CHUNKS):
+        for c, (dc, d, outer, n) in enumerate(CHUNKS):
             o_host = partners(outer)[0]
+            helper = core + 8 * dc + d
+            far, here, ne = masks(dc)
             g.wait_ge(T.sem["ld%d" % c], 32)
             g.remote_dma_fused([
-                RemoteDMATransfer(dst_ids=[dst(on_host(core + d, o_host))], dma_engine_mask=LOW,
+                RemoteDMATransfer(dst_ids=[dst(on_host(helper, o_host))], dma_engine_mask=far,
                                   remote_sem=T.sem["in%d" % c], src=T["g%d" % c][:], dst=T["g%d" % c][:], alu_op=0),
-                RemoteDMATransfer(dst_ids=[dst(core + d)], dma_engine_mask=HIGH,
+                RemoteDMATransfer(dst_ids=[dst(helper)], dma_engine_mask=here,
                                   remote_sem=T.sem["in%d" % c], src=T["k%d" % c][:], dst=T["k%d" % c][:], alu_op=0),
             ], local_sem=T.sem.sent)
+            sent += 2 * ne
         for c, (keep, give) in enumerate(rows):
-            g.sync.wait_ge(T.sem["su%d" % c], 8)
+            ne = masks(CHUNKS[c][0])[2]
+            g.sync.wait_ge(T.sem["su%d" % c], ne)
             g.sync.dma_start(T.y[keep[0]:keep[1], :], T["p%d" % c][:]).then_inc(T.sem.sta, 16)
-            g.scalar.wait_ge(T.sem["sv%d" % c], 8)
+            g.scalar.wait_ge(T.sem["sv%d" % c], ne)
             g.scalar.dma_start(T.y[give[0]:give[1], :], T["q%d" % c][:]).then_inc(T.sem.stb, 16)
-        g.wait_ge(T.sem.sent, 16 * len(CHUNKS))
+        g.wait_ge(T.sem.sent, sent)
         g.sync.wait_ge(T.sem.sta, 16 * len(CHUNKS))
         g.scalar.wait_ge(T.sem.stb, 16 * len(CHUNKS))
         return
 
-    mine = [c for c, ch in enumerate(CHUNKS) if ch[0] == delta]
-    if not mine:
+    jobs = [(r, c) for r in T.cores if topo.host(r) == host
+            for c, ch in enumerate(CHUNKS) if r + 8 * ch[0] + ch[1] == core]
+    if not jobs:
         return
-    for c in mine:
-        i_host = partners(CHUNKS[c][1])[1]
-        g.wait_ge(T.sem["in%d" % c], 16)
+    sent = 0
+    for rank_core, c in jobs:
+        i_host = partners(CHUNKS[c][2])[1]
+        g.wait_ge(T.sem["in%d" % c], 2 * masks(CHUNKS[c][0])[2])
         g.remote_dma_fused([
-            RemoteDMATransfer(dst_ids=[dst(on_host(core, i_host))], dma_engine_mask=LOW,
+            RemoteDMATransfer(dst_ids=[dst(on_host(core, i_host))], dma_engine_mask=0x00FF,
                               remote_sem=T.sem["ps%d" % c], srcs=[T["k%d" % c][:], T["g%d" % c][:]],
                               dsts=[T["p%d" % c][:]], alu_op=1),
         ], local_sem=T.sem.sent)
-    for c in mine:
-        o_host = partners(CHUNKS[c][1])[0]
+        sent += 8
+    for rank_core, c in jobs:
+        o_host = partners(CHUNKS[c][2])[0]
+        far, here, ne = masks(CHUNKS[c][0])
         srcs = [T["k%d" % c][:], T["g%d" % c][:], T["p%d" % c][:]]
         g.wait_ge(T.sem["ps%d" % c], 8)
         g.remote_dma_fused([
-            RemoteDMATransfer(dst_ids=[dst(on_host(rank_core, o_host))], dma_engine_mask=LOW,
+            RemoteDMATransfer(dst_ids=[dst(on_host(rank_core, o_host))], dma_engine_mask=far,
                               remote_sem=T.sem["sv%d" % c], srcs=srcs, dsts=[T["q%d" % c][:]], alu_op=1),
-            RemoteDMATransfer(dst_ids=[dst(rank_core)], dma_engine_mask=HIGH,
+            RemoteDMATransfer(dst_ids=[dst(rank_core)], dma_engine_mask=here,
                               remote_sem=T.sem["su%d" % c], srcs=srcs, dsts=[T["p%d" % c][:]], alu_op=1),
         ], local_sem=T.sem.sent)
-    g.wait_ge(T.sem.sent, 24 * len(mine))
+        sent += 2 * ne
+    g.wait_ge(T.sem.sent, sent)

@@ -1,6 +1,8 @@
 from concourse.bass import DstId, RemoteDMATransfer
 
-CHUNKS = [(2, -2, "s", 10), (2, 1, "s", 10), (4, -2, "s", 11), (4, 1, "s", 11), (0, -2, "s", 11), (0, 1, "s", 11)]
+CHUNKS = [(2, -2, "s", 5), (2, 1, "s", 5), (4, -2, "s", 5), (4, 1, "s", 5), (6, -2, "s", 5), (6, 1, "s", 5),
+          (-2, -2, "s", 5), (-2, 1, "s", 5), (-4, -2, "s", 6), (-4, 1, "s", 6), (0, -2, "s", 6), (0, 1, "s", 6)]
+CALLS = [[c] for c in range(len(CHUNKS))]
 ROWLEN = 1024
 
 SCRATCH = {}
@@ -12,8 +14,31 @@ for ci, chunk in enumerate(CHUNKS):
         SEMAPHORES.append("%s%d" % (nm, ci))
 
 
+def bits(m):
+    return bin(m).count("1")
+
+
 def masks(dchip):
-    return (0x00FF, 0xFF00, 8) if dchip == 0 else (0x000F, 0x00F0, 4)
+    return (0x00FF, 0xFF00) if dchip == 0 else (0x000F, 0x00F0)
+
+
+HOP1 = {}
+for call in CALLS:
+    n_low = sum(1 if CHUNKS[c][0] == 0 else 2 for c in call)
+    n_high = sum(1 for c in call if CHUNKS[c][0] == 0)
+    lo, hi = 0, 8
+    for c in call:
+        w = 8 // n_low
+        far = ((1 << w) - 1) << lo
+        lo += w
+        if CHUNKS[c][0] == 0:
+            v = 8 // n_high
+            here = ((1 << v) - 1) << hi
+            hi += v
+        else:
+            here = ((1 << w) - 1) << lo
+            lo += w
+        HOP1[c] = (far, here)
 
 
 def rank_program(g, core, T, topo):
@@ -40,23 +65,26 @@ def rank_program(g, core, T, topo):
         for c, (keep, give) in enumerate(rows):
             g.sync.dma_start(T["g%d" % c][:], T.x[give[0]:give[1], :]).then_inc(T.sem["ld%d" % c], 16)
             g.scalar.dma_start(T["k%d" % c][:], T.x[keep[0]:keep[1], :]).then_inc(T.sem["ld%d" % c], 16)
-        for c, (dc, d, outer, n) in enumerate(CHUNKS):
-            o_host = partners(outer)[0]
-            helper = core + 8 * dc + d
-            far, here, ne = masks(dc)
-            g.wait_ge(T.sem["ld%d" % c], 32)
-            g.remote_dma_fused([
-                RemoteDMATransfer(dst_ids=[dst(on_host(helper, o_host))], dma_engine_mask=far,
-                                  remote_sem=T.sem["in%d" % c], src=T["g%d" % c][:], dst=T["g%d" % c][:], alu_op=0),
-                RemoteDMATransfer(dst_ids=[dst(helper)], dma_engine_mask=here,
-                                  remote_sem=T.sem["in%d" % c], src=T["k%d" % c][:], dst=T["k%d" % c][:], alu_op=0),
-            ], local_sem=T.sem.sent)
-            sent += 2 * ne
+        for call in CALLS:
+            transfers = []
+            for c in call:
+                dc, d, outer, n = CHUNKS[c]
+                helper = core + 8 * dc + d
+                far, here = HOP1[c]
+                g.wait_ge(T.sem["ld%d" % c], 32)
+                transfers.append(RemoteDMATransfer(
+                    dst_ids=[dst(on_host(helper, partners(outer)[0]))], dma_engine_mask=far,
+                    remote_sem=T.sem["in%d" % c], src=T["g%d" % c][:], dst=T["g%d" % c][:], alu_op=0))
+                transfers.append(RemoteDMATransfer(
+                    dst_ids=[dst(helper)], dma_engine_mask=here,
+                    remote_sem=T.sem["in%d" % c], src=T["k%d" % c][:], dst=T["k%d" % c][:], alu_op=0))
+                sent += bits(far) + bits(here)
+            g.remote_dma_fused(transfers, local_sem=T.sem.sent)
         for c, (keep, give) in enumerate(rows):
-            ne = masks(CHUNKS[c][0])[2]
-            g.sync.wait_ge(T.sem["su%d" % c], ne)
+            far, here = masks(CHUNKS[c][0])
+            g.sync.wait_ge(T.sem["su%d" % c], bits(here))
             g.sync.dma_start(T.y[keep[0]:keep[1], :], T["p%d" % c][:]).then_inc(T.sem.sta, 16)
-            g.scalar.wait_ge(T.sem["sv%d" % c], ne)
+            g.scalar.wait_ge(T.sem["sv%d" % c], bits(far))
             g.scalar.dma_start(T.y[give[0]:give[1], :], T["q%d" % c][:]).then_inc(T.sem.stb, 16)
         g.wait_ge(T.sem.sent, sent)
         g.sync.wait_ge(T.sem.sta, 16 * len(CHUNKS))
@@ -70,7 +98,7 @@ def rank_program(g, core, T, topo):
     sent = 0
     for rank_core, c in jobs:
         i_host = partners(CHUNKS[c][2])[1]
-        g.wait_ge(T.sem["in%d" % c], 2 * masks(CHUNKS[c][0])[2])
+        g.wait_ge(T.sem["in%d" % c], bits(HOP1[c][0]) + bits(HOP1[c][1]))
         g.remote_dma_fused([
             RemoteDMATransfer(dst_ids=[dst(on_host(core, i_host))], dma_engine_mask=0x00FF,
                               remote_sem=T.sem["ps%d" % c], srcs=[T["k%d" % c][:], T["g%d" % c][:]],
@@ -79,7 +107,7 @@ def rank_program(g, core, T, topo):
         sent += 8
     for rank_core, c in jobs:
         o_host = partners(CHUNKS[c][2])[0]
-        far, here, ne = masks(CHUNKS[c][0])
+        far, here = masks(CHUNKS[c][0])
         srcs = [T["k%d" % c][:], T["g%d" % c][:], T["p%d" % c][:]]
         g.wait_ge(T.sem["ps%d" % c], 8)
         g.remote_dma_fused([
@@ -88,5 +116,5 @@ def rank_program(g, core, T, topo):
             RemoteDMATransfer(dst_ids=[dst(rank_core)], dma_engine_mask=here,
                               remote_sem=T.sem["su%d" % c], srcs=srcs, dsts=[T["p%d" % c][:]], alu_op=1),
         ], local_sem=T.sem.sent)
-        sent += 2 * ne
+        sent += bits(far) + bits(here)
     g.wait_ge(T.sem.sent, sent)

@@ -1,7 +1,9 @@
 from concourse.bass import DstId, RemoteDMATransfer
 
-CHUNKS = [(2, -2, "s", 5), (2, 1, "s", 5), (4, -2, "s", 5), (4, 1, "s", 5), (6, -2, "s", 5), (6, 1, "s", 5),
-          (-2, -2, "s", 5), (-2, 1, "s", 5), (-4, -2, "s", 6), (-4, 1, "s", 6), (0, -2, "s", 6), (0, 1, "s", 6)]
+PLACES = [(2, -2), (2, 1), (4, -2), (4, 1), (6, -2), (6, 1), (-2, -2), (-2, 1), (-4, -2), (-4, 1), (-6, -2), (-6, 1),
+          (-8, -2), (0, -2), (0, 1)]
+SIZES = [5, 5, 5, 5, 5, 5, 5, 5, 4, 4, 4, 3, 3, 3, 3]
+CHUNKS = [(PLACES[i][0], PLACES[i][1], "s", SIZES[i]) for i in range(len(SIZES))]
 CALLS = [[c] for c in range(len(CHUNKS))]
 ROWLEN = 1024
 

@@ -1,7 +1,7 @@
 from concourse.bass import DstId, RemoteDMATransfer
 
-PLACES = [(2, -2), (2, 1), (4, -2), (4, 1), (6, -2), (6, 1), (-2, -2), (-2, 1), (-4, -2), (-4, 1), (-6, -2), (-6, 1),
-          (-8, -2), (0, -2), (0, 1)]
+PLACES = [(-1, 0), (2, -2), (2, 1), (4, -2), (4, 1), (-1, 1), (6, -2), (6, 1), (-2, -2), (-2, 1), (-4, -2), (-4, 1),
+          (-6, -2), (0, -2), (0, 1)]
 SIZES = [5, 5, 5, 5, 5, 5, 5, 5, 4, 4, 4, 3, 3, 3, 3]
 CHUNKS = [(PLACES[i][0], PLACES[i][1], "s", SIZES[i]) for i in range(len(SIZES))]
 CALLS = [[c] for c in range(len(CHUNKS))]

from concourse.bass import DstId, RemoteDMATransfer

PLACES = [(-1, 0), (2, -2), (2, 1), (4, -2), (4, 1), (-1, 1), (6, -2), (6, 1), (-2, -2), (-2, 1), (-4, -2), (-4, 1),
          (-6, -2), (0, -2), (0, 1)]
SIZES = [5, 5, 5, 5, 5, 5, 5, 5, 4, 4, 4, 3, 3, 3, 3]
CHUNKS = [(PLACES[i][0], PLACES[i][1], "s", SIZES[i]) for i in range(len(SIZES))]
CALLS = [[c] for c in range(len(CHUNKS))]
ROWLEN = 1024

SCRATCH = {}
SEMAPHORES = ["sent", "sta", "stb"]
for ci, chunk in enumerate(CHUNKS):
    for nm in "kgpq":
        SCRATCH["%s%d" % (nm, ci)] = ("dram", [128, chunk[3] * ROWLEN // 128], "float32")
    for nm in ("ld", "in", "ps", "su", "sv"):
        SEMAPHORES.append("%s%d" % (nm, ci))


def bits(m):
    return bin(m).count("1")


def masks(dchip):
    return (0x00FF, 0xFF00) if dchip == 0 else (0x000F, 0x00F0)


HOP1 = {}
for call in CALLS:
    n_low = sum(1 if CHUNKS[c][0] == 0 else 2 for c in call)
    n_high = sum(1 for c in call if CHUNKS[c][0] == 0)
    lo, hi = 0, 8
    for c in call:
        w = 8 // n_low
        far = ((1 << w) - 1) << lo
        lo += w
        if CHUNKS[c][0] == 0:
            v = 8 // n_high
            here = ((1 << v) - 1) << hi
            hi += v
        else:
            here = ((1 << w) - 1) << lo
            lo += w
        HOP1[c] = (far, here)


def rank_program(g, core, T, topo):
    host = topo.host(core)

    def on_host(c, h):
        return c + (h - host) * 128

    def dst(d):
        rid, pid = topo.addr(d, core)
        return DstId(rid=rid, pnc=pid)

    def partners(outer):
        if outer == "c":
            return 3 - host, host ^ 1, host in (0, 1)
        return host ^ 1, 3 - host, host in (0, 3)

    if T.rank_of(core) is not None:
        rows, r0, sent = [], 0, 0
        for dc, d, outer, n in CHUNKS:
            a, b = (r0, r0 + n), (r0 + n, r0 + 2 * n)
            rows.append((a, b) if partners(outer)[2] else (b, a))
            r0 += 2 * n
        for c, (keep, give) in enumerate(rows):
            g.sync.dma_start(T["g%d" % c][:], T.x[give[0]:give[1], :]).then_inc(T.sem["ld%d" % c], 16)
            g.scalar.dma_start(T["k%d" % c][:], T.x[keep[0]:keep[1], :]).then_inc(T.sem["ld%d" % c], 16)
        for call in CALLS:
            transfers = []
            for c in call:
                dc, d, outer, n = CHUNKS[c]
                helper = core + 8 * dc + d
                far, here = HOP1[c]
                g.wait_ge(T.sem["ld%d" % c], 32)
                transfers.append(RemoteDMATransfer(
                    dst_ids=[dst(on_host(helper, partners(outer)[0]))], dma_engine_mask=far,
                    remote_sem=T.sem["in%d" % c], src=T["g%d" % c][:], dst=T["g%d" % c][:], alu_op=0))
                transfers.append(RemoteDMATransfer(
                    dst_ids=[dst(helper)], dma_engine_mask=here,
                    remote_sem=T.sem["in%d" % c], src=T["k%d" % c][:], dst=T["k%d" % c][:], alu_op=0))
                sent += bits(far) + bits(here)
            g.remote_dma_fused(transfers, local_sem=T.sem.sent)
        for c, (keep, give) in enumerate(rows):
            far, here = masks(CHUNKS[c][0])
            g.sync.wait_ge(T.sem["su%d" % c], bits(here))
            g.sync.dma_start(T.y[keep[0]:keep[1], :], T["p%d" % c][:]).then_inc(T.sem.sta, 16)
            g.scalar.wait_ge(T.sem["sv%d" % c], bits(far))
            g.scalar.dma_start(T.y[give[0]:give[1], :], T["q%d" % c][:]).then_inc(T.sem.stb, 16)
        g.wait_ge(T.sem.sent, sent)
        g.sync.wait_ge(T.sem.sta, 16 * len(CHUNKS))
        g.scalar.wait_ge(T.sem.stb, 16 * len(CHUNKS))
        return

    jobs = [(r, c) for r in T.cores if topo.host(r) == host
            for c, ch in enumerate(CHUNKS) if r + 8 * ch[0] + ch[1] == core]
    if not jobs:
        return
    sent = 0
    for rank_core, c in jobs:
        i_host = partners(CHUNKS[c][2])[1]
        g.wait_ge(T.sem["in%d" % c], bits(HOP1[c][0]) + bits(HOP1[c][1]))
        g.remote_dma_fused([
            RemoteDMATransfer(dst_ids=[dst(on_host(core, i_host))], dma_engine_mask=0x00FF,
                              remote_sem=T.sem["ps%d" % c], srcs=[T["k%d" % c][:], T["g%d" % c][:]],
                              dsts=[T["p%d" % c][:]], alu_op=1),
        ], local_sem=T.sem.sent)
        sent += 8
    for rank_core, c in jobs:
        o_host = partners(CHUNKS[c][2])[0]
        far, here = masks(CHUNKS[c][0])
        srcs = [T["k%d" % c][:], T["g%d" % c][:], T["p%d" % c][:]]
        g.wait_ge(T.sem["ps%d" % c], 8)
        g.remote_dma_fused([
            RemoteDMATransfer(dst_ids=[dst(on_host(rank_core, o_host))], dma_engine_mask=far,
                              remote_sem=T.sem["sv%d" % c], srcs=srcs, dsts=[T["q%d" % c][:]], alu_op=1),
            RemoteDMATransfer(dst_ids=[dst(rank_core)], dma_engine_mask=here,
                              remote_sem=T.sem["su%d" % c], srcs=srcs, dsts=[T["p%d" % c][:]], alu_op=1),
        ], local_sem=T.sem.sent)
        sent += bits(far) + bits(here)
    g.wait_ge(T.sem.sent, sent)
